import numpy as np
CORES = [9,10,11,14,17,18,19,22,49,50,51,54]
N = 12
F = 256
LR = 0.5
def setup_inputs(rng):
    return {"w": rng.standard_normal((N, 128, F), dtype=np.float32) * (0.5 + np.abs(rng.standard_normal((N, 128, 1), dtype=np.float32))), "u": rng.standard_normal((N, 128, F), dtype=np.float32) * (0.5 + np.abs(rng.standard_normal((N, 128, 1), dtype=np.float32)))}
def setup_inputs_big(rng):
    d = setup_inputs(rng)
    for k in ("w", "u"): d[k] = (d[k].astype(np.float32) * 1024.0).astype(d[k].dtype)
    return d
def setup_inputs_small(rng):
    d = setup_inputs(rng)
    for k in ("w", "u"): d[k] = (d[k].astype(np.float32) * (1 / 1024.0)).astype(d[k].dtype)
    return d
def setup_inputs_apart(rng):
    d = setup_inputs(rng)
    f = (10.0 ** rng.permutation(np.linspace(-1.5, 1.5, N))).astype(np.float32).reshape(N, 1, 1)
    for k in ("w", "u"): d[k] = (d[k].astype(np.float32) * f).astype(d[k].dtype)
    return d
def setup_inputs_mixed(rng):
    d = setup_inputs(rng)
    f = (10.0 ** rng.uniform(-3, 3, (1, 128, 1))).astype(np.float32); shape = rng.integers(3, size=(1, 128, 1))
    for k in ("u",):
        x = d[k].astype(np.float32)
        m = x.mean(axis=(0, 2), keepdims=True); level = m + np.sign(x - m) * np.abs(x - m).mean(axis=(0, 2), keepdims=True) * rng.uniform(0.9, 1.1, x.shape).astype(np.float32)
        other = x * np.where(rng.random(x.shape) < 0.5, 0.1, 1.0).astype(np.float32)
        d[k] = (np.where(shape == 1, level, np.where(shape == 2, other, x)) * f).astype(d[k].dtype)
    return d
def reference(w, u):
    W, U = w.astype(np.float64), u.astype(np.float64)
    nw = np.sqrt((W ** 2).sum(axis=(0, 2)).reshape(1, 128, 1))
    nu = np.sqrt((U ** 2).sum(axis=(0, 2)).reshape(1, 128, 1))
    return {"y": (W - LR * (nw / nu) * U).astype(np.float32)}

@@ -1,0 +1,155 @@
+from concourse.bass import DstId, RemoteDMATransfer
+from concourse.mybir import AluOpType, AxisListType, ActivationFunctionType
+
+F = 256
+NA = 96
+ENGINES = 8
+
+SCRATCH = {
+    "wb": ("sbuf", [128, F], "float32"),
+    "ub": ("sbuf", [128, F], "float32"),
+    "sq": ("sbuf", [128, 2 * F], "float32"),
+    "acc": ("sbuf", [128, 16], "float32"),
+    "sj": ("sbuf", [128, 8], "float32"),
+    "tw": ("sbuf", [128, 1], "float32"),
+    "tu": ("sbuf", [128, 1], "float32"),
+    "ru": ("sbuf", [128, 1], "float32"),
+    "cb": ("sbuf", [128, 1], "float32"),
+    "ta": ("psum", [128, 512], "float32"),
+    "tb": ("psum", [128, 512], "float32"),
+    "yb": ("sbuf", [128, F], "float32"),
+}
+SEMAPHORES = ["lw", "lu", "part", "pad", "arr1", "arr2", "sent", "vsum", "ssum", "rec", "coef", "va", "sb", "ydone",
+              "stored"]
+
+
+def _low(mask, n):
+    out, bit, k = 0, 1, 0
+    while k < n:
+        if mask & bit:
+            out |= bit
+            k += 1
+        bit <<= 1
+    return out
+
+
+def _plan(cores, topo):
+    send = {}
+    for ch in sorted({topo.chip(c) for c in cores}):
+        mem = [c for c in cores if topo.chip(c) == ch]
+        dsts = [d for d in cores if topo.chip(d) != ch]
+        elig = {d: [s for s in mem if topo.may_write(s, d)] for d in dsts}
+        cap = 1
+        while True:
+            load = {s: [] for s in mem}
+            ok = True
+            for d in sorted(dsts, key=lambda d: (len(elig[d]), cores.index(d))):
+                cand = [s for s in elig[d] if len(load[s]) < cap]
+                if not cand:
+                    ok = False
+                    break
+                s = min(cand, key=lambda s: (topo.die(s) != topo.die(d), len(load[s]), cores.index(s)))
+                load[s].append(d)
+            if ok:
+                break
+            cap += 1
+        send.update(load)
+    return send
+
+
+def rank_program(g, core, T, topo):
+    if T.rank_of(core) is None:
+        return
+    cores = list(T.cores)
+    sem = T.sem
+    S, V, Q = g.scalar, g.vector, g.sync
+    Act = ActivationFunctionType
+
+    chips = sorted({topo.chip(c) for c in cores})
+    my = topo.chip(core)
+
+    def peers_of(c):
+        return [p for p in cores if topo.chip(p) == topo.chip(c) and p != c]
+
+    def col_part(dst, src):
+        return 4 + 2 * peers_of(dst).index(src)
+
+    def col_sum(dst, src_chip):
+        others = [ch for ch in chips if ch != topo.chip(dst)]
+        return 4 + 2 * len(peers_of(dst)) + 2 * others.index(src_chip)
+
+    peers = peers_of(core)
+    far = [c for c in cores if topo.chip(c) != my]
+    ncols = 4 + 2 * len(peers) + 2 * (len(chips) - 1)
+    plan = _plan(cores, topo)
+
+    mask = 0
+    for c in cores:
+        if c != core:
+            mask = topo.mask(core, c) if mask == 0 else mask & topo.mask(core, c)
+    mask = _low(mask, ENGINES)
+
+    def dst_id(c):
+        rid, pid, _ = topo.addr(c)
+        return DstId(rid=rid, pnc=pid)
+
+    Q.dma_start(T.wb[:], T.w[:]).then_inc(sem.lw, 16)
+    S.dma_start(T.ub[:], T.u[:]).then_inc(sem.lu, 16)
+    V.memset(T.acc[:, 2:4], 0.0).then_inc(sem.pad, 1)
+
+    S.wait_ge(sem.lw, 16)
+    S.activation(T.sq[:, 0:F], T.wb[:], Act.Square, scale=0.5, accum_out=T.acc[:, 0:1]).then_inc(sem.part, 1)
+    S.wait_ge(sem.lu, 16)
+    S.activation(T.sq[:, F:2 * F], T.ub[:], Act.Square, accum_out=T.acc[:, 1:2]).then_inc(sem.part, 1)
+
+    g.wait_ge(sem.part, 2)
+    g.remote_dma_fused([RemoteDMATransfer(
+        dst_ids=[dst_id(p) for p in peers], dma_engine_mask=mask, remote_sem=sem.arr1,
+        srcs=[T.acc[:, 0:2]], dsts=[T.acc[:, col_part(p, core):col_part(p, core) + 2] for p in peers],
+        alu_op=0)], local_sem=sem.sent)
+    sent = ENGINES
+    n1 = ENGINES * len(peers)
+
+    if plan[core]:
+        g.wait_ge(sem.arr1, n1)
+        g.remote_dma_fused([RemoteDMATransfer(
+            dst_ids=[dst_id(d) for d in plan[core]], dma_engine_mask=mask, remote_sem=sem.arr2,
+            srcs=[T.acc[:, 0:2]] + [T.acc[:, 4 + 2 * k:6 + 2 * k] for k in range(len(peers))],
+            dsts=[T.acc[:, col_sum(d, my):col_sum(d, my) + 2] for d in plan[core]],
+            alu_op=1)], local_sem=sem.sent)
+        sent += ENGINES
+    g.wait_ge(sem.sent, sent)
+    n2 = ENGINES * sum(1 for s in far if core in plan[s])
+
+    V.wait_ge(sem.pad, 1)
+    V.wait_ge(sem.part, 2)
+    V.wait_ge(sem.arr1, n1)
+    V.wait_ge(sem.arr2, n2)
+    V.tensor_reduce(T.tu[:], T.acc[:, 1:ncols:2], AxisListType.X, AluOpType.add).then_inc(sem.vsum, 1)
+    V.wait_ge(sem.vsum, 1)
+    V.reciprocal(T.ru[:], T.tu[:]).then_inc(sem.rec, 1)
+
+    S.wait_ge(sem.pad, 1)
+    S.wait_ge(sem.part, 2)
+    S.wait_ge(sem.arr1, n1)
+    S.wait_ge(sem.arr2, n2)
+    S.activation(T.sj[:, 0:ncols // 2], T.acc[:, 0:ncols:2], Act.Copy, accum_out=T.tw[:]).then_inc(sem.ssum, 1)
+    S.wait_ge(sem.ssum, 1)
+    S.wait_ge(sem.rec, 1)
+    S.activation(T.cb[:], T.tw[:], Act.Sqrt, scale=T.ru[:]).then_inc(sem.coef, 1)
+
+    S.wait_ge(sem.coef, 1)
+    S.activation(T.tb[:, 0:F - NA], T.ub[:, NA:F], Act.Identity, scale=T.cb[:]).then_inc(sem.sb, 1)
+
+    V.wait_ge(sem.lw, 16)
+    V.wait_ge(sem.lu, 16)
+    V.wait_ge(sem.coef, 1)
+    V.tensor_scalar(T.ta[:, 0:NA], T.ub[:, 0:NA], T.cb[:], None, AluOpType.mult).then_inc(sem.va, 1)
+    V.wait_ge(sem.va, 1)
+    V.tensor_tensor(T.yb[:, 0:NA], T.wb[:, 0:NA], T.ta[:, 0:NA], AluOpType.subtract).then_inc(sem.ydone, 1)
+    V.wait_ge(sem.sb, 1)
+    V.tensor_tensor(T.yb[:, NA:F], T.wb[:, NA:F], T.tb[:, 0:F - NA], AluOpType.subtract).then_inc(sem.ydone, 1)
+
+    Q.wait_ge(sem.ydone, 2)
+    Q.dma_start(T.y[:], T.yb[:]).then_inc(sem.stored, 16)
+    Q.wait_ge(sem.stored, 16)

@@ -2,25 +2,29 @@ from concourse.bass import DstId, RemoteDMATransfer
 from concourse.mybir import AluOpType, AxisListType, ActivationFunctionType
 
 F = 256
-NA = 96
-ENGINES = 8
+F0 = 64
+FS = 192
+NA = 112
+ENG = 8
 
 SCRATCH = {
     "wb": ("sbuf", [128, F], "float32"),
     "ub": ("sbuf", [128, F], "float32"),
     "sq": ("sbuf", [128, 2 * F], "float32"),
-    "acc": ("sbuf", [128, 16], "float32"),
-    "sj": ("sbuf", [128, 8], "float32"),
+    "acc": ("sbuf", [128, 24], "float32"),
+    "sj": ("sbuf", [128, 12], "float32"),
     "tw": ("sbuf", [128, 1], "float32"),
     "tu": ("sbuf", [128, 1], "float32"),
     "ru": ("sbuf", [128, 1], "float32"),
+    "na": ("sbuf", [128, 1], "float32"),
+    "nb": ("sbuf", [128, 1], "float32"),
     "cb": ("sbuf", [128, 1], "float32"),
     "ta": ("psum", [128, 512], "float32"),
     "tb": ("psum", [128, 512], "float32"),
     "yb": ("sbuf", [128, F], "float32"),
 }
-SEMAPHORES = ["lw", "lu", "part", "pad", "arr1", "arr2", "sent", "vsum", "ssum", "rec", "coef", "va", "sb", "ydone",
-              "stored"]
+SEMAPHORES = ["lw0", "lw1", "lu", "p0", "p1", "pv", "vm", "arr1", "arr2", "sent", "vsum", "ssum", "rec", "ra", "rb",
+              "coef", "va", "sb", "ya", "yz", "stored"]
 
 
 def _low(mask, n):
@@ -31,6 +35,13 @@ def _low(mask, n):
             k += 1
         bit <<= 1
     return out
+
+
+def _common(topo, core, others):
+    mask = topo.mask(core, others[0])
+    for c in others[1:]:
+        mask &= topo.mask(core, c)
+    return mask
 
 
 def _plan(cores, topo):
@@ -64,6 +75,7 @@ def rank_program(g, core, T, topo):
     sem = T.sem
     S, V, Q = g.scalar, g.vector, g.sync
     Act = ActivationFunctionType
+    mult, sub, add = AluOpType.mult, AluOpType.subtract, AluOpType.add
 
     chips = sorted({topo.chip(c) for c in cores})
     my = topo.chip(core)
@@ -72,84 +84,96 @@ def rank_program(g, core, T, topo):
         return [p for p in cores if topo.chip(p) == topo.chip(c) and p != c]
 
     def col_part(dst, src):
-        return 4 + 2 * peers_of(dst).index(src)
+        return 4 + 4 * peers_of(dst).index(src)
 
     def col_sum(dst, src_chip):
         others = [ch for ch in chips if ch != topo.chip(dst)]
-        return 4 + 2 * len(peers_of(dst)) + 2 * others.index(src_chip)
+        return 4 + 4 * len(peers_of(dst)) + 4 * others.index(src_chip)
 
     peers = peers_of(core)
     far = [c for c in cores if topo.chip(c) != my]
-    ncols = 4 + 2 * len(peers) + 2 * (len(chips) - 1)
+    ncols = 4 + 4 * len(peers) + 4 * (len(chips) - 1)
     plan = _plan(cores, topo)
-
-    mask = 0
-    for c in cores:
-        if c != core:
-            mask = topo.mask(core, c) if mask == 0 else mask & topo.mask(core, c)
-    mask = _low(mask, ENGINES)
+    mask = _low(_common(topo, core, peers + far), ENG)
+    n1 = 2 * ENG * len(peers)
+    n2 = ENG * sum(1 for s in far if core in plan[s])
 
     def dst_id(c):
         rid, pid, _ = topo.addr(c)
         return DstId(rid=rid, pnc=pid)
 
-    Q.dma_start(T.wb[:], T.w[:]).then_inc(sem.lw, 16)
+    def step_one(a, b):
+        g.remote_dma_fused([RemoteDMATransfer(
+            dst_ids=[dst_id(p) for p in peers], dma_engine_mask=mask, remote_sem=sem.arr1,
+            srcs=[T.acc[:, a:b]], dsts=[T.acc[:, col_part(p, core) + a:col_part(p, core) + b] for p in peers],
+            alu_op=0)], local_sem=sem.sent)
+
+    Q.dma_start(T.wb[:, 0:F0], T.w[:, 0:F0]).then_inc(sem.lw0, 16)
     S.dma_start(T.ub[:], T.u[:]).then_inc(sem.lu, 16)
-    V.memset(T.acc[:, 2:4], 0.0).then_inc(sem.pad, 1)
+    Q.dma_start(T.wb[:, F0:F], T.w[:, F0:F]).then_inc(sem.lw1, 16)
 
-    S.wait_ge(sem.lw, 16)
-    S.activation(T.sq[:, 0:F], T.wb[:], Act.Square, scale=0.5, accum_out=T.acc[:, 0:1]).then_inc(sem.part, 1)
+    S.wait_ge(sem.lw0, 16)
+    S.activation(T.sq[:, 0:F0], T.wb[:, 0:F0], Act.Square, accum_out=T.acc[:, 0:1]).then_inc(sem.p0, 1)
+    S.wait_ge(sem.lw1, 16)
+    S.activation(T.sq[:, F0:F], T.wb[:, F0:F], Act.Square, accum_out=T.acc[:, 2:3]).then_inc(sem.p1, 1)
     S.wait_ge(sem.lu, 16)
-    S.activation(T.sq[:, F:2 * F], T.ub[:], Act.Square, accum_out=T.acc[:, 1:2]).then_inc(sem.part, 1)
+    S.activation(T.sq[:, F:F + FS], T.ub[:, 0:FS], Act.Square, accum_out=T.acc[:, 1:2]).then_inc(sem.p1, 1)
+    V.wait_ge(sem.lu, 16)
+    V.tensor_tensor(T.sq[:, F + FS:2 * F], T.ub[:, FS:F], T.ub[:, FS:F], mult).then_inc(sem.vm, 1)
+    V.wait_ge(sem.vm, 1)
+    V.tensor_reduce(T.acc[:, 3:4], T.sq[:, F + FS:2 * F], AxisListType.X, add).then_inc(sem.pv, 1)
 
-    g.wait_ge(sem.part, 2)
-    g.remote_dma_fused([RemoteDMATransfer(
-        dst_ids=[dst_id(p) for p in peers], dma_engine_mask=mask, remote_sem=sem.arr1,
-        srcs=[T.acc[:, 0:2]], dsts=[T.acc[:, col_part(p, core):col_part(p, core) + 2] for p in peers],
-        alu_op=0)], local_sem=sem.sent)
-    sent = ENGINES
-    n1 = ENGINES * len(peers)
+    g.wait_ge(sem.p0, 1)
+    step_one(0, 1)
+    g.wait_ge(sem.p1, 2)
+    g.wait_ge(sem.pv, 1)
+    step_one(1, 4)
+    sent = 2 * ENG
 
     if plan[core]:
         g.wait_ge(sem.arr1, n1)
         g.remote_dma_fused([RemoteDMATransfer(
             dst_ids=[dst_id(d) for d in plan[core]], dma_engine_mask=mask, remote_sem=sem.arr2,
-            srcs=[T.acc[:, 0:2]] + [T.acc[:, 4 + 2 * k:6 + 2 * k] for k in range(len(peers))],
-            dsts=[T.acc[:, col_sum(d, my):col_sum(d, my) + 2] for d in plan[core]],
+            srcs=[T.acc[:, 4 * k:4 * k + 4] for k in range(1 + len(peers))],
+            dsts=[T.acc[:, col_sum(d, my):col_sum(d, my) + 4] for d in plan[core]],
             alu_op=1)], local_sem=sem.sent)
-        sent += ENGINES
+        sent += ENG
     g.wait_ge(sem.sent, sent)
-    n2 = ENGINES * sum(1 for s in far if core in plan[s])
 
-    V.wait_ge(sem.pad, 1)
-    V.wait_ge(sem.part, 2)
-    V.wait_ge(sem.arr1, n1)
-    V.wait_ge(sem.arr2, n2)
-    V.tensor_reduce(T.tu[:], T.acc[:, 1:ncols:2], AxisListType.X, AluOpType.add).then_inc(sem.vsum, 1)
+    for E in (S, V):
+        E.wait_ge(sem.p0, 1)
+        E.wait_ge(sem.p1, 2)
+        E.wait_ge(sem.pv, 1)
+        E.wait_ge(sem.arr1, n1)
+        E.wait_ge(sem.arr2, n2)
+    S.activation(T.sj[:, 0:ncols // 2], T.acc[:, 0:ncols:2], Act.Copy, scale=0.25,
+                 accum_out=T.tw[:]).then_inc(sem.ssum, 1)
+    S.wait_ge(sem.ssum, 1)
+    S.activation(T.na[:], T.tw[:], Act.Sqrt).then_inc(sem.ra, 1)
+    V.tensor_reduce(T.tu[:], T.acc[:, 1:ncols:2], AxisListType.X, add).then_inc(sem.vsum, 1)
     V.wait_ge(sem.vsum, 1)
     V.reciprocal(T.ru[:], T.tu[:]).then_inc(sem.rec, 1)
-
-    S.wait_ge(sem.pad, 1)
-    S.wait_ge(sem.part, 2)
-    S.wait_ge(sem.arr1, n1)
-    S.wait_ge(sem.arr2, n2)
-    S.activation(T.sj[:, 0:ncols // 2], T.acc[:, 0:ncols:2], Act.Copy, accum_out=T.tw[:]).then_inc(sem.ssum, 1)
-    S.wait_ge(sem.ssum, 1)
     S.wait_ge(sem.rec, 1)
-    S.activation(T.cb[:], T.tw[:], Act.Sqrt, scale=T.ru[:]).then_inc(sem.coef, 1)
+    S.activation(T.nb[:], T.ru[:], Act.Sqrt).then_inc(sem.rb, 1)
 
+    S.wait_ge(sem.ra, 1)
+    S.wait_ge(sem.rb, 1)
+    S.activation(T.cb[:], T.na[:], Act.Identity, scale=T.nb[:]).then_inc(sem.coef, 1)
     S.wait_ge(sem.coef, 1)
     S.activation(T.tb[:, 0:F - NA], T.ub[:, NA:F], Act.Identity, scale=T.cb[:]).then_inc(sem.sb, 1)
 
-    V.wait_ge(sem.lw, 16)
-    V.wait_ge(sem.lu, 16)
-    V.wait_ge(sem.coef, 1)
-    V.tensor_scalar(T.ta[:, 0:NA], T.ub[:, 0:NA], T.cb[:], None, AluOpType.mult).then_inc(sem.va, 1)
+    V.wait_ge(sem.lw0, 16)
+    V.wait_ge(sem.lw1, 16)
+    V.wait_ge(sem.ra, 1)
+    V.wait_ge(sem.rb, 1)
+    V.tensor_scalar(T.ta[:, 0:NA], T.ub[:, 0:NA], T.na[:], T.nb[:], mult, mult).then_inc(sem.va, 1)
     V.wait_ge(sem.va, 1)
-    V.tensor_tensor(T.yb[:, 0:NA], T.wb[:, 0:NA], T.ta[:, 0:NA], AluOpType.subtract).then_inc(sem.ydone, 1)
+    V.tensor_tensor(T.yb[:, 0:NA], T.wb[:, 0:NA], T.ta[:, 0:NA], sub).then_inc(sem.ya, 1)
     V.wait_ge(sem.sb, 1)
-    V.tensor_tensor(T.yb[:, NA:F], T.wb[:, NA:F], T.tb[:, 0:F - NA], AluOpType.subtract).then_inc(sem.ydone, 1)
+    V.tensor_tensor(T.yb[:, NA:F], T.wb[:, NA:F], T.tb[:, 0:F - NA], sub).then_inc(sem.yz, 1)
 
-    Q.wait_ge(sem.ydone, 2)
-    Q.dma_start(T.y[:], T.yb[:]).then_inc(sem.stored, 16)
-    Q.wait_ge(sem.stored, 16)
+    Q.wait_ge(sem.ya, 1)
+    Q.dma_start(T.y[:, 0:NA], T.yb[:, 0:NA]).then_inc(sem.stored, 16)
+    Q.wait_ge(sem.yz, 1)
+    Q.dma_start(T.y[:, NA:F], T.yb[:, NA:F]).then_inc(sem.stored, 16)
+    Q.wait_ge(sem.stored, 32)

@@ -4,27 +4,35 @@ from concourse.mybir import AluOpType, AxisListType, ActivationFunctionType
 F = 256
 F0 = 64
 FS = 192
-NA = 112
+NA = 64
+NB = 128
 ENG = 8
+TINY = 1e-30
 
 SCRATCH = {
     "wb": ("sbuf", [128, F], "float32"),
     "ub": ("sbuf", [128, F], "float32"),
+    "uk": ("sbuf", [128, F], "float32"),
     "sq": ("sbuf", [128, 2 * F], "float32"),
     "acc": ("sbuf", [128, 24], "float32"),
-    "sj": ("sbuf", [128, 12], "float32"),
-    "tw": ("sbuf", [128, 1], "float32"),
-    "tu": ("sbuf", [128, 1], "float32"),
+    "sj": ("sbuf", [128, 24], "float32"),
+    "pp": ("sbuf", [128, 2], "float32"),
+    "mm": ("sbuf", [128, 2], "float32"),
+    "ss": ("sbuf", [128, 2], "float32"),
+    "iv": ("sbuf", [128, 2], "float32"),
+    "rw": ("sbuf", [128, 1], "float32"),
     "ru": ("sbuf", [128, 1], "float32"),
-    "na": ("sbuf", [128, 1], "float32"),
-    "nb": ("sbuf", [128, 1], "float32"),
-    "cb": ("sbuf", [128, 1], "float32"),
+    "xx": ("sbuf", [128, 1], "float32"),
+    "yy": ("sbuf", [128, 1], "float32"),
+    "ry": ("sbuf", [128, 1], "float32"),
+    "rr": ("sbuf", [128, 1], "float32"),
     "ta": ("psum", [128, 512], "float32"),
     "tb": ("psum", [128, 512], "float32"),
+    "tc": ("psum", [128, 512], "float32"),
     "yb": ("sbuf", [128, F], "float32"),
 }
-SEMAPHORES = ["lw0", "lw1", "lu", "p0", "p1", "pv", "vm", "arr1", "arr2", "sent", "vsum", "ssum", "rec", "ra", "rb",
-              "coef", "va", "sb", "ya", "yz", "stored"]
+SEMAPHORES = ["lw0", "lw1", "lu", "p0", "p1", "pv", "vm", "arr1", "arr2", "sent", "e1", "e2", "e3", "e4", "e5", "e6",
+              "sy", "sx", "rec", "root", "va", "sb1", "sb2", "ya", "yz", "stored"]
 
 
 def _low(mask, n):
@@ -93,6 +101,7 @@ def rank_program(g, core, T, topo):
     peers = peers_of(core)
     far = [c for c in cores if topo.chip(c) != my]
     ncols = 4 + 4 * len(peers) + 4 * (len(chips) - 1)
+    half = ncols // 2
     plan = _plan(cores, topo)
     mask = _low(_common(topo, core, peers + far), ENG)
     n1 = 2 * ENG * len(peers)
@@ -144,36 +153,51 @@ def rank_program(g, core, T, topo):
         E.wait_ge(sem.p0, 1)
         E.wait_ge(sem.p1, 2)
         E.wait_ge(sem.pv, 1)
-        E.wait_ge(sem.arr1, n1)
-        E.wait_ge(sem.arr2, n2)
-    S.activation(T.sj[:, 0:ncols // 2], T.acc[:, 0:ncols:2], Act.Copy, scale=0.25,
-                 accum_out=T.tw[:]).then_inc(sem.ssum, 1)
-    S.wait_ge(sem.ssum, 1)
-    S.activation(T.na[:], T.tw[:], Act.Sqrt).then_inc(sem.ra, 1)
-    V.tensor_reduce(T.tu[:], T.acc[:, 1:ncols:2], AxisListType.X, add).then_inc(sem.vsum, 1)
-    V.wait_ge(sem.vsum, 1)
-    V.reciprocal(T.ru[:], T.tu[:]).then_inc(sem.rec, 1)
-    S.wait_ge(sem.rec, 1)
-    S.activation(T.nb[:], T.ru[:], Act.Sqrt).then_inc(sem.rb, 1)
+    V.tensor_tensor(T.pp[:], T.acc[:, 0:2], T.acc[:, 2:4], add).then_inc(sem.e1, 1)
+    V.wait_ge(sem.e1, 1)
+    V.tensor_scalar(T.mm[:], T.pp[:], TINY, None, AluOpType.is_lt).then_inc(sem.e2, 1)
+    V.wait_ge(sem.e2, 1)
+    V.tensor_tensor(T.ss[:], T.pp[:], T.mm[:], AluOpType.max).then_inc(sem.e3, 1)
+    V.wait_ge(sem.e3, 1)
+    V.reciprocal(T.iv[:], T.ss[:]).then_inc(sem.e4, 1)
+    S.wait_ge(sem.e3, 1)
+    S.activation(T.rw[:], T.ss[:, 0:1], Act.Sqrt, scale=0.25).then_inc(sem.e5, 1)
+    S.wait_ge(sem.e4, 1)
+    S.activation(T.ru[:], T.iv[:, 1:2], Act.Sqrt).then_inc(sem.e5, 1)
+    V.wait_ge(sem.e5, 2)
+    V.tensor_scalar(T.uk[:], T.ub[:], T.rw[:], T.ru[:], mult, mult).then_inc(sem.e6, 1)
 
-    S.wait_ge(sem.ra, 1)
-    S.wait_ge(sem.rb, 1)
-    S.activation(T.cb[:], T.na[:], Act.Identity, scale=T.nb[:]).then_inc(sem.coef, 1)
-    S.wait_ge(sem.coef, 1)
-    S.activation(T.tb[:, 0:F - NA], T.ub[:, NA:F], Act.Identity, scale=T.cb[:]).then_inc(sem.sb, 1)
+    S.wait_ge(sem.arr1, n1)
+    S.wait_ge(sem.arr2, n2)
+    S.activation(T.sj[:, 0:half], T.acc[:, 1:ncols:2], Act.Identity, scale=T.iv[:, 1:2],
+                 accum_out=T.yy[:]).then_inc(sem.sy, 1)
+    S.activation(T.sj[:, half:2 * half], T.acc[:, 0:ncols:2], Act.Identity, scale=T.iv[:, 0:1],
+                 accum_out=T.xx[:]).then_inc(sem.sx, 1)
+    V.wait_ge(sem.sy, 1)
+    V.reciprocal(T.ry[:], T.yy[:]).then_inc(sem.rec, 1)
+    S.wait_ge(sem.sx, 1)
+    S.wait_ge(sem.rec, 1)
+    S.activation(T.rr[:], T.xx[:], Act.Sqrt, scale=T.ry[:]).then_inc(sem.root, 1)
+
+    S.wait_ge(sem.root, 1)
+    S.wait_ge(sem.e6, 1)
+    S.activation(T.tb[:, 0:NB - NA], T.uk[:, NA:NB], Act.Identity, scale=T.rr[:]).then_inc(sem.sb1, 1)
+    S.activation(T.tc[:, 0:F - NB], T.uk[:, NB:F], Act.Identity, scale=T.rr[:]).then_inc(sem.sb2, 1)
 
     V.wait_ge(sem.lw0, 16)
     V.wait_ge(sem.lw1, 16)
-    V.wait_ge(sem.ra, 1)
-    V.wait_ge(sem.rb, 1)
-    V.tensor_scalar(T.ta[:, 0:NA], T.ub[:, 0:NA], T.na[:], T.nb[:], mult, mult).then_inc(sem.va, 1)
+    V.wait_ge(sem.e6, 1)
+    V.wait_ge(sem.root, 1)
+    V.tensor_scalar(T.ta[:, 0:NA], T.uk[:, 0:NA], T.rr[:], None, mult).then_inc(sem.va, 1)
+    V.wait_ge(sem.sb1, 1)
+    V.tensor_tensor(T.yb[:, NA:NB], T.wb[:, NA:NB], T.tb[:, 0:NB - NA], sub).then_inc(sem.ya, 1)
     V.wait_ge(sem.va, 1)
     V.tensor_tensor(T.yb[:, 0:NA], T.wb[:, 0:NA], T.ta[:, 0:NA], sub).then_inc(sem.ya, 1)
-    V.wait_ge(sem.sb, 1)
-    V.tensor_tensor(T.yb[:, NA:F], T.wb[:, NA:F], T.tb[:, 0:F - NA], sub).then_inc(sem.yz, 1)
+    V.wait_ge(sem.sb2, 1)
+    V.tensor_tensor(T.yb[:, NB:F], T.wb[:, NB:F], T.tc[:, 0:F - NB], sub).then_inc(sem.yz, 1)
 
-    Q.wait_ge(sem.ya, 1)
-    Q.dma_start(T.y[:, 0:NA], T.yb[:, 0:NA]).then_inc(sem.stored, 16)
+    Q.wait_ge(sem.ya, 2)
+    Q.dma_start(T.y[:, 0:NB], T.yb[:, 0:NB]).then_inc(sem.stored, 16)
     Q.wait_ge(sem.yz, 1)
-    Q.dma_start(T.y[:, NA:F], T.yb[:, NA:F]).then_inc(sem.stored, 16)
+    Q.dma_start(T.y[:, NB:F], T.yb[:, NB:F]).then_inc(sem.stored, 16)
     Q.wait_ge(sem.stored, 32)

@@ -2,7 +2,7 @@ from concourse.bass import DstId, RemoteDMATransfer
 from concourse.mybir import AluOpType, AxisListType, ActivationFunctionType
 
 F = 256
-F0 = 64
+F0 = 16
 FS = 192
 NA = 64
 NB = 128
@@ -14,8 +14,8 @@ SCRATCH = {
     "ub": ("sbuf", [128, F], "float32"),
     "uk": ("sbuf", [128, F], "float32"),
     "sq": ("sbuf", [128, 2 * F], "float32"),
-    "acc": ("sbuf", [128, 24], "float32"),
-    "sj": ("sbuf", [128, 24], "float32"),
+    "acc": ("sbuf", [128, 32], "float32"),
+    "sj": ("sbuf", [128, 32], "float32"),
     "pp": ("sbuf", [128, 2], "float32"),
     "mm": ("sbuf", [128, 2], "float32"),
     "ss": ("sbuf", [128, 2], "float32"),
@@ -43,6 +43,14 @@ def _low(mask, n):
             k += 1
         bit <<= 1
     return out
+
+
+def _count(mask):
+    k = 0
+    while mask:
+        k += mask & 1
+        mask >>= 1
+    return k
 
 
 def _common(topo, core, others):
@@ -96,15 +104,18 @@ def rank_program(g, core, T, topo):
 
     def col_sum(dst, src_chip):
         others = [ch for ch in chips if ch != topo.chip(dst)]
-        return 4 + 4 * len(peers_of(dst)) + 4 * others.index(src_chip)
+        return 4 + 4 * len(peers_of(dst)) + 8 * others.index(src_chip)
 
     peers = peers_of(core)
     far = [c for c in cores if topo.chip(c) != my]
-    ncols = 4 + 4 * len(peers) + 4 * (len(chips) - 1)
+    nown = 4 + 4 * len(peers)
+    ncols = nown + 8 * (len(chips) - 1)
     half = ncols // 2
     plan = _plan(cores, topo)
-    mask = _low(_common(topo, core, peers + far), ENG)
-    n1 = 2 * ENG * len(peers)
+    mask1 = _common(topo, core, peers)
+    eng1 = _count(mask1)
+    mask2 = _low(_common(topo, core, peers + far), ENG)
+    n1 = 2 * eng1 * len(peers)
     n2 = ENG * sum(1 for s in far if core in plan[s])
 
     def dst_id(c):
@@ -113,13 +124,13 @@ def rank_program(g, core, T, topo):
 
     def step_one(a, b):
         g.remote_dma_fused([RemoteDMATransfer(
-            dst_ids=[dst_id(p) for p in peers], dma_engine_mask=mask, remote_sem=sem.arr1,
+            dst_ids=[dst_id(p) for p in peers], dma_engine_mask=mask1, remote_sem=sem.arr1,
             srcs=[T.acc[:, a:b]], dsts=[T.acc[:, col_part(p, core) + a:col_part(p, core) + b] for p in peers],
             alu_op=0)], local_sem=sem.sent)
 
     Q.dma_start(T.wb[:, 0:F0], T.w[:, 0:F0]).then_inc(sem.lw0, 16)
-    S.dma_start(T.ub[:], T.u[:]).then_inc(sem.lu, 16)
     Q.dma_start(T.wb[:, F0:F], T.w[:, F0:F]).then_inc(sem.lw1, 16)
+    Q.dma_start(T.ub[:], T.u[:]).then_inc(sem.lu, 16)
 
     S.wait_ge(sem.lw0, 16)
     S.activation(T.sq[:, 0:F0], T.wb[:, 0:F0], Act.Square, accum_out=T.acc[:, 0:1]).then_inc(sem.p0, 1)
@@ -137,14 +148,14 @@ def rank_program(g, core, T, topo):
     g.wait_ge(sem.p1, 2)
     g.wait_ge(sem.pv, 1)
     step_one(1, 4)
-    sent = 2 * ENG
+    sent = 2 * eng1
 
     if plan[core]:
         g.wait_ge(sem.arr1, n1)
         g.remote_dma_fused([RemoteDMATransfer(
-            dst_ids=[dst_id(d) for d in plan[core]], dma_engine_mask=mask, remote_sem=sem.arr2,
-            srcs=[T.acc[:, 4 * k:4 * k + 4] for k in range(1 + len(peers))],
-            dsts=[T.acc[:, col_sum(d, my):col_sum(d, my) + 4] for d in plan[core]],
+            dst_ids=[dst_id(d) for d in plan[core]], dma_engine_mask=mask2, remote_sem=sem.arr2,
+            srcs=[T.acc[:, 0:nown // 2], T.acc[:, nown // 2:nown]],
+            dsts=[T.acc[:, col_sum(d, my):col_sum(d, my) + 8] for d in plan[core]],
             alu_op=1)], local_sem=sem.sent)
         sent += ENG
     g.wait_ge(sem.sent, sent)

from concourse.bass import DstId, RemoteDMATransfer
from concourse.mybir import AluOpType, AxisListType, ActivationFunctionType

F = 256
F0 = 16
FS = 192
NA = 64
NB = 128
ENG = 8
TINY = 1e-30

SCRATCH = {
    "wb": ("sbuf", [128, F], "float32"),
    "ub": ("sbuf", [128, F], "float32"),
    "uk": ("sbuf", [128, F], "float32"),
    "sq": ("sbuf", [128, 2 * F], "float32"),
    "acc": ("sbuf", [128, 32], "float32"),
    "sj": ("sbuf", [128, 32], "float32"),
    "pp": ("sbuf", [128, 2], "float32"),
    "mm": ("sbuf", [128, 2], "float32"),
    "ss": ("sbuf", [128, 2], "float32"),
    "iv": ("sbuf", [128, 2], "float32"),
    "rw": ("sbuf", [128, 1], "float32"),
    "ru": ("sbuf", [128, 1], "float32"),
    "xx": ("sbuf", [128, 1], "float32"),
    "yy": ("sbuf", [128, 1], "float32"),
    "ry": ("sbuf", [128, 1], "float32"),
    "rr": ("sbuf", [128, 1], "float32"),
    "ta": ("psum", [128, 512], "float32"),
    "tb": ("psum", [128, 512], "float32"),
    "tc": ("psum", [128, 512], "float32"),
    "yb": ("sbuf", [128, F], "float32"),
}
SEMAPHORES = ["lw0", "lw1", "lu", "p0", "p1", "pv", "vm", "arr1", "arr2", "sent", "e1", "e2", "e3", "e4", "e5", "e6",
              "sy", "sx", "rec", "root", "va", "sb1", "sb2", "ya", "yz", "stored"]


def _low(mask, n):
    out, bit, k = 0, 1, 0
    while k < n:
        if mask & bit:
            out |= bit
            k += 1
        bit <<= 1
    return out


def _count(mask):
    k = 0
    while mask:
        k += mask & 1
        mask >>= 1
    return k


def _common(topo, core, others):
    mask = topo.mask(core, others[0])
    for c in others[1:]:
        mask &= topo.mask(core, c)
    return mask


def _plan(cores, topo):
    send = {}
    for ch in sorted({topo.chip(c) for c in cores}):
        mem = [c for c in cores if topo.chip(c) == ch]
        dsts = [d for d in cores if topo.chip(d) != ch]
        elig = {d: [s for s in mem if topo.may_write(s, d)] for d in dsts}
        cap = 1
        while True:
            load = {s: [] for s in mem}
            ok = True
            for d in sorted(dsts, key=lambda d: (len(elig[d]), cores.index(d))):
                cand = [s for s in elig[d] if len(load[s]) < cap]
                if not cand:
                    ok = False
                    break
                s = min(cand, key=lambda s: (topo.die(s) != topo.die(d), len(load[s]), cores.index(s)))
                load[s].append(d)
            if ok:
                break
            cap += 1
        send.update(load)
    return send


def rank_program(g, core, T, topo):
    if T.rank_of(core) is None:
        return
    cores = list(T.cores)
    sem = T.sem
    S, V, Q = g.scalar, g.vector, g.sync
    Act = ActivationFunctionType
    mult, sub, add = AluOpType.mult, AluOpType.subtract, AluOpType.add

    chips = sorted({topo.chip(c) for c in cores})
    my = topo.chip(core)

    def peers_of(c):
        return [p for p in cores if topo.chip(p) == topo.chip(c) and p != c]

    def col_part(dst, src):
        return 4 + 4 * peers_of(dst).index(src)

    def col_sum(dst, src_chip):
        others = [ch for ch in chips if ch != topo.chip(dst)]
        return 4 + 4 * len(peers_of(dst)) + 8 * others.index(src_chip)

    peers = peers_of(core)
    far = [c for c in cores if topo.chip(c) != my]
    nown = 4 + 4 * len(peers)
    ncols = nown + 8 * (len(chips) - 1)
    half = ncols // 2
    plan = _plan(cores, topo)
    mask1 = _common(topo, core, peers)
    eng1 = _count(mask1)
    mask2 = _low(_common(topo, core, peers + far), ENG)
    n1 = 2 * eng1 * len(peers)
    n2 = ENG * sum(1 for s in far if core in plan[s])

    def dst_id(c):
        rid, pid, _ = topo.addr(c)
        return DstId(rid=rid, pnc=pid)

    def step_one(a, b):
        g.remote_dma_fused([RemoteDMATransfer(
            dst_ids=[dst_id(p) for p in peers], dma_engine_mask=mask1, remote_sem=sem.arr1,
            srcs=[T.acc[:, a:b]], dsts=[T.acc[:, col_part(p, core) + a:col_part(p, core) + b] for p in peers],
            alu_op=0)], local_sem=sem.sent)

    Q.dma_start(T.wb[:, 0:F0], T.w[:, 0:F0]).then_inc(sem.lw0, 16)
    Q.dma_start(T.wb[:, F0:F], T.w[:, F0:F]).then_inc(sem.lw1, 16)
    Q.dma_start(T.ub[:], T.u[:]).then_inc(sem.lu, 16)

    S.wait_ge(sem.lw0, 16)
    S.activation(T.sq[:, 0:F0], T.wb[:, 0:F0], Act.Square, accum_out=T.acc[:, 0:1]).then_inc(sem.p0, 1)
    S.wait_ge(sem.lw1, 16)
    S.activation(T.sq[:, F0:F], T.wb[:, F0:F], Act.Square, accum_out=T.acc[:, 2:3]).then_inc(sem.p1, 1)
    S.wait_ge(sem.lu, 16)
    S.activation(T.sq[:, F:F + FS], T.ub[:, 0:FS], Act.Square, accum_out=T.acc[:, 1:2]).then_inc(sem.p1, 1)
    V.wait_ge(sem.lu, 16)
    V.tensor_tensor(T.sq[:, F + FS:2 * F], T.ub[:, FS:F], T.ub[:, FS:F], mult).then_inc(sem.vm, 1)
    V.wait_ge(sem.vm, 1)
    V.tensor_reduce(T.acc[:, 3:4], T.sq[:, F + FS:2 * F], AxisListType.X, add).then_inc(sem.pv, 1)

    g.wait_ge(sem.p0, 1)
    step_one(0, 1)
    g.wait_ge(sem.p1, 2)
    g.wait_ge(sem.pv, 1)
    step_one(1, 4)
    sent = 2 * eng1

    if plan[core]:
        g.wait_ge(sem.arr1, n1)
        g.remote_dma_fused([RemoteDMATransfer(
            dst_ids=[dst_id(d) for d in plan[core]], dma_engine_mask=mask2, remote_sem=sem.arr2,
            srcs=[T.acc[:, 0:nown // 2], T.acc[:, nown // 2:nown]],
            dsts=[T.acc[:, col_sum(d, my):col_sum(d, my) + 8] for d in plan[core]],
            alu_op=1)], local_sem=sem.sent)
        sent += ENG
    g.wait_ge(sem.sent, sent)

    for E in (S, V):
        E.wait_ge(sem.p0, 1)
        E.wait_ge(sem.p1, 2)
        E.wait_ge(sem.pv, 1)
    V.tensor_tensor(T.pp[:], T.acc[:, 0:2], T.acc[:, 2:4], add).then_inc(sem.e1, 1)
    V.wait_ge(sem.e1, 1)
    V.tensor_scalar(T.mm[:], T.pp[:], TINY, None, AluOpType.is_lt).then_inc(sem.e2, 1)
    V.wait_ge(sem.e2, 1)
    V.tensor_tensor(T.ss[:], T.pp[:], T.mm[:], AluOpType.max).then_inc(sem.e3, 1)
    V.wait_ge(sem.e3, 1)
    V.reciprocal(T.iv[:], T.ss[:]).then_inc(sem.e4, 1)
    S.wait_ge(sem.e3, 1)
    S.activation(T.rw[:], T.ss[:, 0:1], Act.Sqrt, scale=0.25).then_inc(sem.e5, 1)
    S.wait_ge(sem.e4, 1)
    S.activation(T.ru[:], T.iv[:, 1:2], Act.Sqrt).then_inc(sem.e5, 1)
    V.wait_ge(sem.e5, 2)
    V.tensor_scalar(T.uk[:], T.ub[:], T.rw[:], T.ru[:], mult, mult).then_inc(sem.e6, 1)

    S.wait_ge(sem.arr1, n1)
    S.wait_ge(sem.arr2, n2)
    S.activation(T.sj[:, 0:half], T.acc[:, 1:ncols:2], Act.Identity, scale=T.iv[:, 1:2],
                 accum_out=T.yy[:]).then_inc(sem.sy, 1)
    S.activation(T.sj[:, half:2 * half], T.acc[:, 0:ncols:2], Act.Identity, scale=T.iv[:, 0:1],
                 accum_out=T.xx[:]).then_inc(sem.sx, 1)
    V.wait_ge(sem.sy, 1)
    V.reciprocal(T.ry[:], T.yy[:]).then_inc(sem.rec, 1)
    S.wait_ge(sem.sx, 1)
    S.wait_ge(sem.rec, 1)
    S.activation(T.rr[:], T.xx[:], Act.Sqrt, scale=T.ry[:]).then_inc(sem.root, 1)

    S.wait_ge(sem.root, 1)
    S.wait_ge(sem.e6, 1)
    S.activation(T.tb[:, 0:NB - NA], T.uk[:, NA:NB], Act.Identity, scale=T.rr[:]).then_inc(sem.sb1, 1)
    S.activation(T.tc[:, 0:F - NB], T.uk[:, NB:F], Act.Identity, scale=T.rr[:]).then_inc(sem.sb2, 1)

    V.wait_ge(sem.lw0, 16)
    V.wait_ge(sem.lw1, 16)
    V.wait_ge(sem.e6, 1)
    V.wait_ge(sem.root, 1)
    V.tensor_scalar(T.ta[:, 0:NA], T.uk[:, 0:NA], T.rr[:], None, mult).then_inc(sem.va, 1)
    V.wait_ge(sem.sb1, 1)
    V.tensor_tensor(T.yb[:, NA:NB], T.wb[:, NA:NB], T.tb[:, 0:NB - NA], sub).then_inc(sem.ya, 1)
    V.wait_ge(sem.va, 1)
    V.tensor_tensor(T.yb[:, 0:NA], T.wb[:, 0:NA], T.ta[:, 0:NA], sub).then_inc(sem.ya, 1)
    V.wait_ge(sem.sb2, 1)
    V.tensor_tensor(T.yb[:, NB:F], T.wb[:, NB:F], T.tc[:, 0:F - NB], sub).then_inc(sem.yz, 1)

    Q.wait_ge(sem.ya, 2)
    Q.dma_start(T.y[:, 0:NB], T.yb[:, 0:NB]).then_inc(sem.stored, 16)
    Q.wait_ge(sem.yz, 1)
    Q.dma_start(T.y[:, NB:F], T.yb[:, NB:F]).then_inc(sem.stored, 16)
    Q.wait_ge(sem.stored, 32)
